import numpy as np, ml_dtypes
CORES = [33,38,57,62,81,86,161,166,185,190,209,214]
N = 12
import mx_ref
NC, G, S2 = 256, 4, 2
C = np.float32(0.019)
CNT = [[0,64,24,24,0,40,0,0,48,32,0,24],[56,56,16,16,56,16,16,0,8,0,0,16],[0,16,0,0,48,16,0,32,56,24,48,16],[32,16,16,0,32,32,32,40,0,40,16,0],[48,0,88,32,24,24,0,16,0,24,0,0],[32,0,16,56,0,0,80,0,0,48,24,0],[0,40,0,16,0,64,24,8,24,0,16,64],[0,24,40,0,16,0,0,48,32,40,56,0],[0,0,24,80,32,0,8,64,0,0,0,48],[0,40,16,32,16,48,32,0,32,0,16,24],[0,0,16,0,32,16,16,32,16,32,32,64],[88,0,0,0,0,0,48,16,40,16,48,0]]
OFF = [[sum(c[:e]) for e in range(N + 1)] for c in CNT]
BF = ml_dtypes.bfloat16
def cut(t, i, w=512):
    return t[:, w * i:w * i + w]
def tile(rs):
    return np.stack(rs, axis=2).reshape(128, -1).astype(BF)
def layer(w, X):
    out = []
    for i in range(G):
        for t in range(len(X)):
            p = mx_ref.matmul(mx_ref.quantize(cut(w, len(X) * i + t)), X[t])
            z = p if t == 0 else z + p
        out.append(z)
    return out
def act(Z):
    return [np.maximum(z, 0) * C for z in Z]
def setup_inputs(rng):
    def f(*shape):
        return mx_ref.flush((rng.standard_normal(shape, dtype=np.float32) * np.exp2(rng.integers(-2, 3, shape[:-1] + (1,)))).astype(BF))
    gt = (0.125 + 0.875 * rng.random((N, 2, NC))).astype(BF)
    return {"gt": gt, "x": f(N, 128, 4 * NC), "w1": f(N, 128, G * 512), "w2": f(N, 128, 512)}
def setup_inputs_blocks(rng):
    d = setup_inputs(rng)
    for k in ("x", "w1", "w2"): d[k] = mx_ref.spread(d[k], rng, 4)
    return d
def setup_inputs_wide(rng):
    d = setup_inputs(rng)
    for k in ("x", "w1", "w2"): d[k] = mx_ref.flush((d[k].astype(np.float32) * np.exp2(rng.integers(-8, 9, (N, 1, 1))).astype(np.float32)).astype(BF))
    return d
def setup_inputs_zeros(rng):
    d = setup_inputs(rng); v = d["x"].reshape(N, 128, -1, 4).copy()
    v[np.broadcast_to((rng.random((N, 1, v.shape[2], 1)) < 0.33), v.shape)] = 0
    d["x"] = v.reshape(d["x"].shape)
    return d
def reference(gt, x, w1, w2):
    y = np.zeros((N, 128, NC), np.float32); g = gt.astype(np.float32)
    for e in range(N):
        f = (e - S2) % N
        t = np.concatenate([x[j][:, 4 * OFF[j][k]:4 * OFF[j][k + 1]] for k in (e, f) for j in range(N)], axis=1)
        p = mx_ref.matmul(mx_ref.quantize(w2[e]), mx_ref.quantize(tile(act(layer(w1[e], [mx_ref.quantize(t)])))))
        c = 0
        for i, k in enumerate((e, f)):
            for j in range(N):
                a, b = OFF[j][k], OFF[j][k + 1]
                y[j][:, a:b] = y[j][:, a:b] + p[:, c:c + b - a] * g[j, i, a:b]; c += b - a
    return {"y": y}

@@ -1,0 +1,364 @@
+from concourse.bass import DstId, RemoteDMATransfer
+from concourse.mybir import dt, AluOpType, ActivationFunctionType
+
+N, NC, ALL = 12, 256, 256
+NK = N // 2
+GAIN = 0.019
+BYTES = dt.uint8
+Q8, U8, BF, F4 = "float8_e4m3fn_x4", "uint8", "bfloat16", "float32"
+SCRATCH = {
+    "xt": ("sbuf", [128, 4 * 384], BF),
+    "xq": ("sbuf", [128, 384], Q8), "xp": ("sbuf", [128, 384], U8),
+    "rq": ("sbuf", [128, 384], Q8), "rp": ("sbuf", [128, 384], U8),
+    "lq": ("sbuf", [128, 640], Q8), "lp": ("sbuf", [128, 640], U8),
+    "w1t": ("sbuf", [128, 2048], BF), "w2t": ("sbuf", [128, 512], BF),
+    "wq0": ("sbuf", [128, 640], Q8), "wp0": ("sbuf", [128, 640], U8),
+    "wq1": ("sbuf", [128, 640], Q8), "wp1": ("sbuf", [128, 640], U8),
+    "h0": ("sbuf", [128, 2048], BF), "h1": ("sbuf", [128, 2048], BF),
+    "hq0": ("sbuf", [128, 512], Q8), "hp0": ("sbuf", [128, 512], U8),
+    "hq1": ("sbuf", [128, 512], Q8), "hp1": ("sbuf", [128, 512], U8),
+    "zp": ("psum", [128, 4096], F4),
+    "pr": ("sbuf", [128, 512], F4),
+    "yl": ("sbuf", [128, 512], F4),
+    "g1": ("sbuf", [128, 512], BF), "gb": ("sbuf", [128, 512], BF),
+    "t1": ("sbuf", [128, 256], F4), "t2": ("sbuf", [128, 256], F4), "yo": ("sbuf", [128, 256], F4),
+}
+SEMAPHORES = (["lx", "lw1", "lw2", "lg", "gb", "qx", "qo", "qw", "rc", "rp", "xa", "w0", "w1", "ls", "m", "yd", "st", "es"]
+              + ["z%d%d" % (s, i) for s in range(2) for i in range(4)]
+              + [n + str(s) for n in ("hv", "hs", "hq", "p") for s in range(2)]
+              + ["ev%d" % k for k in range(4)] + ["y%d" % k for k in range(NK)])
+CACHE = {}
+
+
+def bits(mask):
+    return [1 << b for b in range(mask.bit_length()) if mask >> b & 1]
+
+
+def codes(ap):
+    return ap.bitcast(BYTES)
+
+
+def up16(v):
+    return (v + 15) // 16 * 16
+
+
+def plan(T, topo):
+    if CACHE:
+        return CACHE
+    cores, cnt = list(T.cores), T.tables["CNT"]
+
+    def same_chip(a, b):
+        return (topo.host(a), topo.chip(a)) == (topo.host(b), topo.chip(b))
+
+    def owner(c):
+        return all(topo.may_write(c, d) for d in cores if d != c)
+
+    def helpers(c):
+        return [d for d in range(ALL) if same_chip(c, d) and d not in cores and topo.die(d) == topo.die(c) and owner(d)]
+
+    pair = [[c[2 * k] + c[2 * k + 1] for k in range(NK)] for c in cnt]
+    wrap = [p[-1] for p in pair]
+    tot = [NC + w for w in wrap]
+    start = [[sum(([wrap[j]] + pair[j])[:k]) for k in range(NK)] for j in range(N)]
+    width = [[pair[j][k - 1] + pair[j][k] for k in range(NK)] for j in range(N)]
+    pos = [[sum(width[j][:k]) for k in range(NK)] for j in range(N)]
+
+    comp, dest = {}, {}
+    for k in range(NK):
+        a, b = cores[2 * k], cores[2 * k + 1]
+        cc = [a, helpers(a)[0], b, helpers(b)[0]]
+        others = sorted([j for j in range(N) if j // 2 != k and width[j][k]], key=lambda j: -width[j][k])
+        load = {a: width[2 * k][k], b: width[2 * k + 1][k], cc[1]: 0, cc[3]: 0}
+        room = {a: 2, b: 2, cc[1]: 3, cc[3]: 3}
+        best, pick = [10 ** 6, None], {}
+
+        def search(i):
+            if max(load.values()) >= best[0]:
+                return
+            if i == len(others):
+                best[0], best[1] = max(load.values()), dict(pick)
+                return
+            j = others[i]
+            for d in cc:
+                if room[d] and topo.may_write(d, cores[j]):
+                    room[d] -= 1
+                    load[d] += width[j][k]
+                    pick[j] = d
+                    search(i + 1)
+                    room[d] += 1
+                    load[d] -= width[j][k]
+        search(0)
+        for d in cc:
+            lead = a if topo.die(d) == topo.die(a) else b
+            comp[d] = {"k": k, "own": cores.index(d) if d in cores else None, "lead": cores.index(lead) % 2,
+                       "from": [j for j in sorted(others) if best[1][j] == d]}
+        for j in others:
+            dest[j, k] = best[1][j]
+
+    relay, direct, via = {}, {}, {}
+    for j in range(N):
+        c = cores[j]
+        away = [k for k in range(NK) if k != j // 2 and width[j][k]]
+        plane = [k for k in away if topo.same_plane(c, cores[2 * k])]
+        cross = [k for k in away if k not in plane]
+        hl = helpers(c)
+        relay[j] = [(hl[0], k) for k in cross[:2]] if owner(c) else [(hl[i % len(hl)], k) for i, k in enumerate(cross)]
+        direct[j] = [k for k in plane + cross if k not in [kk for h, kk in relay[j]]]
+        for k in direct[j]:
+            via[j, k] = c
+        for h, k in relay[j]:
+            via[j, k] = h
+
+    send = {}
+    for d, q in comp.items():
+        k, own, col, land = q["k"], q["own"], 0, []
+        q["lo"] = 0
+        if own is not None:
+            w, s = width[own][k], start[own][k]
+            m = max(128, up16(w))
+            ahead = s + w >= m
+            if ahead:
+                q["fill"], q["lo"], col = (0, s + w - m, m), m - w, m
+                land.append((own, m - w))
+        for i, j in enumerate(q["from"]):
+            s, n, lead = start[j][k], width[j][k], 0
+            if own is not None and not ahead and i == len(q["from"]) - 1 and (col + n) % 16:
+                lead = 0 if s + n + 8 <= tot[j] else 8
+                s, n = s - lead, n + 8
+            send[j, k] = (s, n, col)
+            land.append((j, col + lead))
+            col += n
+        if own is not None and not ahead:
+            q["fill"] = (col, s0(start, own, k), max(128, up16(width[own][k])))
+            assert col % 16 == 0 and q["fill"][1] + q["fill"][2] <= tot[own]
+            land.append((own, col))
+            col += width[own][k]
+        q["n"] = col - q["lo"]
+        assert 128 <= q["n"] <= 512
+        q["land"] = [(j, c - q["lo"]) for j, c in land]
+
+    span, skip = {}, {}
+    for j in range(N):
+        hs = [h for i, (h, k) in enumerate(relay[j]) if h not in [x for x, y in relay[j][:i]]]
+        lo = {h: min(send[j, k][0] for x, k in relay[j] if x == h) for h in hs}
+        hi = {h: max(send[j, k][0] + send[j, k][1] for x, k in relay[j] if x == h) for h in hs}
+        w = max(hi[h] - lo[h] for h in hs)
+        span[j] = [(h, min(lo[h], tot[j] - w), w) for h in hs]
+        for h, s, w in span[j]:
+            for x, k in relay[j]:
+                if x == h:
+                    skip[j, k] = send[j, k][0] - s
+
+    def runs(j, k):
+        out, c = [], 0
+        for i, r in enumerate((2 * k - 2, 2 * k - 1, 2 * k, 2 * k + 1)):
+            n = cnt[j][r % N]
+            if n:
+                out.append((c, n, i % 2))
+            c += n
+        return out
+
+    CACHE.update(cores=cores, pair=pair, wrap=wrap, tot=tot, start=start, width=width, pos=pos, runs=runs, comp=comp, dest=dest,
+                 relay=relay, direct=direct, via=via, send=send, span=span, skip=skip)
+    return CACHE
+
+
+def s0(start, j, k):
+    return start[j][k]
+
+
+def weight_dests(core, P, topo):
+    k = P["comp"][core]["k"]
+    ds = [d for d, q in P["comp"].items() if q["k"] == k and d != core]
+    return [d for d in ds if topo.die(d) == topo.die(core)], [d for d in ds if topo.die(d) != topo.die(core)]
+
+
+def engine_halves(core, P, topo):
+    out = [d for d in P["cores"] if d != core and topo.may_write(core, d)
+           and (topo.host(d), topo.chip(d)) != (topo.host(core), topo.chip(core))][0]
+    lo = bits(topo.mask(core, out))
+    return lo, [b for b in bits(topo.mask(core, weight_dests(core, P, topo)[0][0])) if b not in lo]
+
+
+def rank_program(g, core, T, topo):
+    P = plan(T, topo)
+    rank, sent = T.rank_of(core), [0]
+
+    def push(dst, out, src, sem):
+        m = topo.mask(core, dst)
+        rid, pid = topo.addr(dst, core)
+        g.remote_dma(out, src, sem, T.sem.ls, pid, rid, m)
+        sent[0] += len(bits(m))
+
+    def fused(items):
+        tr = []
+        for dsts, src, sem, eng in items:
+            ids = []
+            for d, o in dsts:
+                rid, pid = topo.addr(d, core)
+                ids.append(DstId(rid=rid, pnc=pid))
+            tr.append(RemoteDMATransfer(dst_ids=ids, dma_engine_mask=sum(eng), remote_sem=sem, srcs=[src], dsts=[o for d, o in dsts]))
+            sent[0] += len(eng)
+        g.remote_dma_fused(tr, local_sem=T.sem.ls)
+
+    if rank is not None:
+        send_side(g, core, rank, T, P, push, fused, topo)
+    helping = [(j, k) for (j, k), h in P["via"].items() if h == core and j != rank]
+    if helping:
+        relay_side(g, T, P, helping, push, topo)
+    if core in P["comp"]:
+        compute_side(g, core, rank, T, P, push, topo)
+    if rank is not None:
+        combine_side(g, rank, T, P, topo)
+    if sent[0]:
+        g.wait_ge(T.sem.ls, sent[0])
+
+
+def send_side(g, core, rank, T, P, push, fused, topo):
+    S, tot, wrap, par = T.sem, P["tot"][rank], P["wrap"][rank], rank % 2
+    g.sync.dma_start(T.xt[:, 4 * wrap:4 * tot], T.x[:]).then_inc(S.lx, 16)
+    if wrap:
+        g.sync.dma_start(T.xt[:, 0:4 * wrap], T.x[:, 4 * (NC - wrap):4 * NC]).then_inc(S.lx, 16)
+    g.sync.dma_start(T.w1t[:], T.w1[:]).then_inc(S.lw1, 16)
+    g.sync.dma_start(T.w2t[:], T.w2[:]).then_inc(S.lw2, 16)
+    g.scalar.dma_start(T.g1[0:1, 0:NC], T.gt[0:1, :]).then_inc(S.lg, 16)
+    g.scalar.dma_start(T.g1[0:1, NC:2 * NC], T.gt[1:2, :]).then_inc(S.lg, 16)
+
+    v = g.vector
+    v.wait_ge(S.lx, 32 if wrap else 16)
+    v.quantize_mx(T.xq[:, 0:tot], T.xp[:, 0:tot], T.xt[:, 0:4 * tot]).then_inc(S.qx, 1)
+    p, s, m = P["comp"][core]["fill"]
+    v.quantize_mx(T.lq[:, p:p + m], T.lp[:, p:p + m], T.xt[:, 4 * s:4 * (s + m)]).then_inc(S.qo, 1)
+    wq, wp = T["wq%d" % par], T["wp%d" % par]
+    v.wait_ge(S.lw1, 16)
+    v.quantize_mx(wq[:, 0:512], wp[:, 0:512], T.w1t[:]).then_inc(S.qw, 1)
+    v.wait_ge(S.lw2, 16)
+    v.quantize_mx(wq[:, 512:640], wp[:, 512:640], T.w2t[:]).then_inc(S.qw, 1)
+
+    g.wait_ge(S.qx, 1)
+    sp = P["span"][rank]
+    eng = bits(topo.mask(core, sp[0][0]))
+    per = len(eng) // len(sp)
+    fused([([(h, codes(T.rq[:, 0:w]))], codes(T.xq[:, s:s + w]), S.rc, eng[i * per:i * per + per]) for i, (h, s, w) in enumerate(sp)])
+    fused([([(h, T.rp[:, 0:w])], T.xp[:, s:s + w], S.rp, eng[i * per:i * per + per]) for i, (h, s, w) in enumerate(sp)])
+
+    def windows(ks):
+        for k in ks:
+            s, w, c = P["send"][rank, k]
+            d = P["dest"][rank, k]
+            push(d, codes(T.lq[:, c:c + w]), codes(T.xq[:, s:s + w]), S.xa)
+            push(d, T.lp[:, c:c + w], T.xp[:, s:s + w], S.xa)
+    windows(P["direct"][rank][:1])
+    g.wait_ge(S.qw, 2)
+    near, far = weight_dests(core, P, topo)
+    lo, hi = engine_halves(core, P, topo)
+    sem = S["w%d" % par]
+    fused([([(d, codes(wq[:])) for d in far], codes(wq[:]), sem, hi), ([(d, codes(wq[:])) for d in near], codes(wq[:]), sem, lo)])
+    fused([([(d, wp[:]) for d in far], wp[:], sem, hi), ([(d, wp[:]) for d in near], wp[:], sem, lo)])
+    windows(P["direct"][rank][1:])
+    g.wait_ge(S.lg, 32)
+    g.partition_broadcast(T.gb[:], T.g1[0:1, :], 128).then_inc(S.gb, 1)
+
+
+def relay_side(g, T, P, helping, push, topo):
+    S, j = T.sem, helping[0][0]
+    n = len(bits(topo.mask(P["cores"][j], P["span"][j][0][0]))) // len(P["span"][j])
+    g.wait_ge(S.rc, n)
+    for j, k in helping:
+        a, (_, w, c), d = P["skip"][j, k], P["send"][j, k], P["dest"][j, k]
+        push(d, codes(T.lq[:, c:c + w]), codes(T.rq[:, a:a + w]), S.xa)
+    g.wait_ge(S.rp, n)
+    for j, k in helping:
+        a, (_, w, c), d = P["skip"][j, k], P["send"][j, k], P["dest"][j, k]
+        push(d, T.lp[:, c:c + w], T.rp[:, a:a + w], S.xa)
+
+
+def compute_side(g, core, rank, T, P, push, topo):
+    S, q, cores, w = T.sem, P["comp"][core], P["cores"], P["width"]
+    k, n, lo = q["k"], q["n"], q["lo"]
+    order = (q["lead"], 1 - q["lead"])
+    te, ve, sc = g.tensor, g.vector, g.scalar
+    arr = sum(2 * len(bits(topo.mask(P["via"][j, k], core))) for j in q["from"])
+    x, xs = T.lq[:, lo:lo + n], T.lp[:, lo:lo + n]
+    for s, e in enumerate(order):
+        wq, wp = T["wq%d" % e], T["wp%d" % e]
+        src = cores[2 * k + e]
+        if src == core:
+            te.wait_ge(S.qw, 2)
+        else:
+            a, b = engine_halves(src, P, topo)
+            te.wait_ge(S["w%d" % e], 2 * len(a if core in weight_dests(src, P, topo)[0] else b))
+        if s == 0:
+            if rank is not None:
+                te.wait_ge(S.qo, 1)
+            te.wait_ge(S.xa, arr)
+        for i in range(4):
+            o = 512 * (4 * s + i)
+            te.matmul_mx(T.zp[:, o:o + n], wq[:, 128 * i:128 * i + 128], wp[:, 128 * i:128 * i + 128], x, xs, True, True).then_inc(S["z%d%d" % (s, i)], 1)
+    for s, e in enumerate(order):
+        h, hq, hp = T["h%d" % s], T["hq%d" % s], T["hp%d" % s]
+        for i in range(4):
+            o = 512 * (4 * s + i)
+            out, z, sem = h[:, i:4 * n:4], T.zp[:, o:o + n], S["z%d%d" % (s, i)]
+            if i % 2 == s:
+                ve.wait_ge(sem, 1)
+                ve.tensor_scalar(out, z, 0.0, GAIN, AluOpType.max, AluOpType.mult).then_inc(S["hv%d" % s], 1)
+            else:
+                sc.wait_ge(sem, 1)
+                sc.activation(out, z, ActivationFunctionType.Relu, scale=GAIN).then_inc(S["hs%d" % s], 1)
+        ve.wait_ge(S["hv%d" % s], 2)
+        ve.wait_ge(S["hs%d" % s], 2)
+        ve.quantize_mx(hq[:, 0:n], hp[:, 0:n], h[:, 0:4 * n]).then_inc(S["hq%d" % s], 1)
+        te.wait_ge(S["hq%d" % s], 1)
+        te.matmul_mx(T.zp[:, 2048 * s:2048 * s + n], T["wq%d" % e][:, 512:640], T["wp%d" % e][:, 512:640], hq[:, 0:n], hp[:, 0:n], True, True).then_inc(S["p%d" % s], 1)
+    far = [t for t in q["land"] if t[0] != rank]
+    own = [t for t in q["land"] if t[0] == rank]
+    a, b = min(c for j, c in far), max(c + w[j][k] for j, c in far)
+    sc.wait_ge(S.p0, 1)
+    sc.activation(T.pr[:, a:b], T.zp[:, a:b], ActivationFunctionType.Copy).then_inc(S.es, 1)
+    for j, c in own:
+        o = P["pos"][j][k]
+        sc.activation(T.yl[:, o:o + w[j][k]], T.zp[:, c:c + w[j][k]], ActivationFunctionType.Copy).then_inc(S.es, 1)
+    ve.wait_ge(S.es, 1 + len(own))
+    ve.wait_ge(S.p1, 1)
+    g.wait_ge(S.es, 1 + len(own))
+    for i, (j, c) in enumerate(far + own):
+        o, cnt = P["pos"][j][k], 0
+        for r, m, e in P["runs"](j, k):
+            if e == order[1]:
+                out = T.yl[:, o + r:o + r + m] if j == rank else T.pr[:, c + r:c + r + m]
+                ve.tensor_copy(out, T.zp[:, 2048 + c + r:2048 + c + r + m]).then_inc(S["ev%d" % i], 1)
+                cnt += 1
+        if cnt:
+            (ve if j == rank else g).wait_ge(S["ev%d" % i], cnt)
+        if j != rank:
+            push(cores[j], T.yl[:, o:o + w[j][k]], T.pr[:, c:c + w[j][k]], S["y%d" % k])
+
+
+def combine_side(g, rank, T, P, topo):
+    S, v, k0, pair, cores = T.sem, g.vector, rank // 2, P["pair"][rank], P["cores"]
+    off = [sum(pair[:i]) for i in range(NK)]
+    v.wait_ge(S.gb, 1)
+    have, nm, nadd = [0] * NK, 0, 0
+    for k in [k0] + [k for k in range(NK) if k != k0]:
+        if k != k0 and P["width"][rank][k]:
+            v.wait_ge(S["y%d" % k], len(bits(topo.mask(P["dest"][rank, k], cores[rank]))))
+        a, done = P["pos"][rank][k], []
+        for second, pk in ((1, (k - 1) % NK), (0, k)):
+            n, o = pair[pk], off[pk]
+            have[pk] += 1
+            if n:
+                t = T.t2 if second else T.t1
+                v.tensor_tensor(t[:, o:o + n], T.yl[:, a:a + n], T.gb[:, NC * second + o:NC * second + o + n], AluOpType.mult).then_inc(S.m, 1)
+                nm += 1
+                a += n
+                if have[pk] == 2:
+                    done.append((o, n))
+        if done:
+            v.wait_ge(S.m, nm)
+        for o, n in done:
+            v.tensor_tensor(T.yo[:, o:o + n], T.t1[:, o:o + n], T.t2[:, o:o + n], AluOpType.add).then_inc(S.yd, 1)
+            nadd += 1
+    g.sync.wait_ge(S.yd, nadd)
+    g.sync.dma_start(T.y[:], T.yo[:]).then_inc(S.st, 16)
+    g.sync.wait_ge(S.st, 16)

@@ -6,6 +6,7 @@ NK = N // 2
 GAIN = 0.019
 BYTES = dt.uint8
 Q8, U8, BF, F4 = "float8_e4m3fn_x4", "uint8", "bfloat16", "float32"
+VE = ((0, 2), (1, 3))
 SCRATCH = {
     "xt": ("sbuf", [128, 4 * 384], BF),
     "xq": ("sbuf", [128, 384], Q8), "xp": ("sbuf", [128, 384], U8),
@@ -20,10 +21,12 @@ SCRATCH = {
     "zp": ("psum", [128, 4096], F4),
     "pr": ("sbuf", [128, 512], F4),
     "yl": ("sbuf", [128, 512], F4),
-    "g1": ("sbuf", [128, 512], BF), "gb": ("sbuf", [128, 512], BF),
-    "t1": ("sbuf", [128, 256], F4), "t2": ("sbuf", [128, 256], F4), "yo": ("sbuf", [128, 256], F4),
+    "yo": ("sbuf", [128, 256], F4),
+    "gd": ("dram", [128, 4], BF), "gf": ("dram", [128, 4], BF),
+    "gi0": ("dram", [128, 4], BF), "gi1": ("dram", [128, 4], BF), "gi2": ("dram", [128, 4], BF),
+    "gr": ("sbuf", [128, 512], BF), "gw": ("sbuf", [128, 512], BF),
 }
-SEMAPHORES = (["lx", "lw1", "lw2", "lg", "gb", "qx", "qo", "qw", "rc", "rp", "xa", "w0", "w1", "ls", "m", "yd", "st", "es"]
+SEMAPHORES = (["lx", "lw1", "lw2", "ld", "lg", "gb", "gf", "ga", "qx", "qo", "qw", "rc", "rp", "xa", "w0", "w1", "ls", "yd", "st", "es"]
               + ["z%d%d" % (s, i) for s in range(2) for i in range(4)]
               + [n + str(s) for n in ("hv", "hs", "hq", "p") for s in range(2)]
               + ["ev%d" % k for k in range(4)] + ["y%d" % k for k in range(NK)])
@@ -64,6 +67,7 @@ def plan(T, topo):
     pos = [[sum(width[j][:k]) for k in range(NK)] for j in range(N)]
 
     comp, dest = {}, {}
+    entry = {(k, x): 0 for k in range(NK) for x in {topo.die(c) for c in cores}}
     for k in range(NK):
         a, b = cores[2 * k], cores[2 * k + 1]
         cc = [a, helpers(a)[0], b, helpers(b)[0]]
@@ -73,20 +77,23 @@ def plan(T, topo):
         best, pick = [10 ** 6, None], {}
 
         def search(i):
-            if max(load.values()) >= best[0]:
+            cost = max(load.values()) + max(entry.values())
+            if cost >= best[0]:
                 return
             if i == len(others):
-                best[0], best[1] = max(load.values()), dict(pick)
+                best[0], best[1] = cost, dict(pick)
                 return
             j = others[i]
             for d in cc:
-                if room[d] and topo.may_write(d, cores[j]):
+                if room[d] and topo.may_write(d, cores[j]) and (d not in cores or topo.may_write(cores[j], d)):
                     room[d] -= 1
                     load[d] += width[j][k]
+                    entry[j // 2, topo.die(d)] += width[j][k]
                     pick[j] = d
                     search(i + 1)
                     room[d] += 1
                     load[d] -= width[j][k]
+                    entry[j // 2, topo.die(d)] -= width[j][k]
         search(0)
         for d in cc:
             lead = a if topo.die(d) == topo.die(a) else b
@@ -94,6 +101,7 @@ def plan(T, topo):
                        "from": [j for j in sorted(others) if best[1][j] == d]}
         for j in others:
             dest[j, k] = best[1][j]
+            entry[j // 2, topo.die(best[1][j])] += width[j][k]
 
     relay, direct, via = {}, {}, {}
     for j in range(N):
@@ -108,6 +116,7 @@ def plan(T, topo):
             via[j, k] = c
         for h, k in relay[j]:
             via[j, k] = h
+    gvia = {(j, k): cores[j] if dest[j, k] in cores else via[j, k] for j, k in via}
 
     send = {}
     for d, q in comp.items():
@@ -129,10 +138,11 @@ def plan(T, topo):
             land.append((j, col + lead))
             col += n
         if own is not None and not ahead:
-            q["fill"] = (col, s0(start, own, k), max(128, up16(width[own][k])))
-            assert col % 16 == 0 and q["fill"][1] + q["fill"][2] <= tot[own]
+            s, n = start[own][k], width[own][k]
+            q["fill"] = (col, s, max(128, up16(n)))
+            assert col % 16 == 0 and s + q["fill"][2] <= tot[own]
             land.append((own, col))
-            col += width[own][k]
+            col += n
         q["n"] = col - q["lo"]
         assert 128 <= q["n"] <= 512
         q["land"] = [(j, c - q["lo"]) for j, c in land]
@@ -159,12 +169,8 @@ def plan(T, topo):
         return out
 
     CACHE.update(cores=cores, pair=pair, wrap=wrap, tot=tot, start=start, width=width, pos=pos, runs=runs, comp=comp, dest=dest,
-                 relay=relay, direct=direct, via=via, send=send, span=span, skip=skip)
+                 relay=relay, direct=direct, via=via, gvia=gvia, send=send, span=span, skip=skip)
     return CACHE
-
-
-def s0(start, j, k):
-    return start[j][k]
 
 
 def weight_dests(core, P, topo):
@@ -205,7 +211,7 @@ def rank_program(g, core, T, topo):
         send_side(g, core, rank, T, P, push, fused, topo)
     helping = [(j, k) for (j, k), h in P["via"].items() if h == core and j != rank]
     if helping:
-        relay_side(g, T, P, helping, push, topo)
+        relay_side(g, core, T, P, helping, push, fused, topo)
     if core in P["comp"]:
         compute_side(g, core, rank, T, P, push, topo)
     if rank is not None:
@@ -214,15 +220,23 @@ def rank_program(g, core, T, topo):
         g.wait_ge(T.sem.ls, sent[0])
 
 
+def gate_slots(T, P, j, core):
+    out = []
+    for k in range(NK):
+        if P["gvia"].get((j, k)) == core:
+            d = P["dest"][j, k]
+            out.append((d, T["gi%d" % P["comp"][d]["from"].index(j)][:]))
+    return out
+
+
 def send_side(g, core, rank, T, P, push, fused, topo):
     S, tot, wrap, par = T.sem, P["tot"][rank], P["wrap"][rank], rank % 2
+    g.scalar.dma_start(T.gd[:], T.gt[:]).then_inc(S.ld, 16)
     g.sync.dma_start(T.xt[:, 4 * wrap:4 * tot], T.x[:]).then_inc(S.lx, 16)
     if wrap:
         g.sync.dma_start(T.xt[:, 0:4 * wrap], T.x[:, 4 * (NC - wrap):4 * NC]).then_inc(S.lx, 16)
     g.sync.dma_start(T.w1t[:], T.w1[:]).then_inc(S.lw1, 16)
     g.sync.dma_start(T.w2t[:], T.w2[:]).then_inc(S.lw2, 16)
-    g.scalar.dma_start(T.g1[0:1, 0:NC], T.gt[0:1, :]).then_inc(S.lg, 16)
-    g.scalar.dma_start(T.g1[0:1, NC:2 * NC], T.gt[1:2, :]).then_inc(S.lg, 16)
 
     v = g.vector
     v.wait_ge(S.lx, 32 if wrap else 16)
@@ -235,8 +249,12 @@ def send_side(g, core, rank, T, P, push, fused, topo):
     v.wait_ge(S.lw2, 16)
     v.quantize_mx(wq[:, 512:640], wp[:, 512:640], T.w2t[:]).then_inc(S.qw, 1)
 
+    lo, hi = engine_halves(core, P, topo)
+    direct, sp = P["direct"][rank], P["span"][rank]
+    near, far = [(h, T.gf[:]) for h, s, w in sp if gate_slots(T, P, rank, h)], gate_slots(T, P, rank, core)
+    g.wait_ge(S.ld, 16)
+    fused(([(far, T.gd[:], S.ga, lo)] if far else []) + ([(near, T.gd[:], S.gf, hi)] if near else []))
     g.wait_ge(S.qx, 1)
-    sp = P["span"][rank]
     eng = bits(topo.mask(core, sp[0][0]))
     per = len(eng) // len(sp)
     fused([([(h, codes(T.rq[:, 0:w]))], codes(T.xq[:, s:s + w]), S.rc, eng[i * per:i * per + per]) for i, (h, s, w) in enumerate(sp)])
@@ -248,21 +266,23 @@ def send_side(g, core, rank, T, P, push, fused, topo):
             d = P["dest"][rank, k]
             push(d, codes(T.lq[:, c:c + w]), codes(T.xq[:, s:s + w]), S.xa)
             push(d, T.lp[:, c:c + w], T.xp[:, s:s + w], S.xa)
-    windows(P["direct"][rank][:1])
+    windows(direct[:1])
     g.wait_ge(S.qw, 2)
     near, far = weight_dests(core, P, topo)
-    lo, hi = engine_halves(core, P, topo)
     sem = S["w%d" % par]
     fused([([(d, codes(wq[:])) for d in far], codes(wq[:]), sem, hi), ([(d, codes(wq[:])) for d in near], codes(wq[:]), sem, lo)])
     fused([([(d, wp[:]) for d in far], wp[:], sem, hi), ([(d, wp[:]) for d in near], wp[:], sem, lo)])
-    windows(P["direct"][rank][1:])
-    g.wait_ge(S.lg, 32)
-    g.partition_broadcast(T.gb[:], T.g1[0:1, :], 128).then_inc(S.gb, 1)
+    windows(direct[1:])
 
 
-def relay_side(g, T, P, helping, push, topo):
+def relay_side(g, core, T, P, helping, push, fused, topo):
     S, j = T.sem, helping[0][0]
-    n = len(bits(topo.mask(P["cores"][j], P["span"][j][0][0]))) // len(P["span"][j])
+    src = P["cores"][j]
+    n = len(bits(topo.mask(src, core))) // len(P["span"][j])
+    slots = gate_slots(T, P, j, core)
+    if slots:
+        g.wait_ge(S.gf, len(engine_halves(src, P, topo)[1]))
+        fused([(slots, T.gf[:], S.ga, bits(topo.mask(core, slots[0][0])))])
     g.wait_ge(S.rc, n)
     for j, k in helping:
         a, (_, w, c), d = P["skip"][j, k], P["send"][j, k], P["dest"][j, k]
@@ -279,6 +299,22 @@ def compute_side(g, core, rank, T, P, push, topo):
     order = (q["lead"], 1 - q["lead"])
     te, ve, sc = g.tensor, g.vector, g.scalar
     arr = sum(2 * len(bits(topo.mask(P["via"][j, k], core))) for j in q["from"])
+    cnt = 0
+    for j, c in sorted(q["land"], key=lambda t: t[0] != rank):
+        if j == rank:
+            src = T.gd
+            g.sync.wait_ge(S.ld, 16)
+        else:
+            src = T["gi%d" % q["from"].index(j)]
+            if j == q["from"][0]:
+                g.sync.wait_ge(S.ga, sum(len(bits(topo.mask(P["gvia"][i, k], core))) for i in q["from"]))
+        for which, pk in ((1, (k - 1) % NK), (0, k)):
+            m = P["pair"][j][pk]
+            if m:
+                r = (NC * which + sum(P["pair"][j][:pk])) // 4
+                g.sync.dma_start(T.gr[0:1, c:c + m], src[r:r + m // 4, :]).then_inc(S.lg, 16)
+                c += m
+                cnt += 1
     x, xs = T.lq[:, lo:lo + n], T.lp[:, lo:lo + n]
     for s, e in enumerate(order):
         wq, wp = T["wq%d" % e], T["wp%d" % e]
@@ -300,34 +336,52 @@ def compute_side(g, core, rank, T, P, push, topo):
         for i in range(4):
             o = 512 * (4 * s + i)
             out, z, sem = h[:, i:4 * n:4], T.zp[:, o:o + n], S["z%d%d" % (s, i)]
-            if i % 2 == s:
+            if i in VE[s]:
                 ve.wait_ge(sem, 1)
                 ve.tensor_scalar(out, z, 0.0, GAIN, AluOpType.max, AluOpType.mult).then_inc(S["hv%d" % s], 1)
             else:
                 sc.wait_ge(sem, 1)
                 sc.activation(out, z, ActivationFunctionType.Relu, scale=GAIN).then_inc(S["hs%d" % s], 1)
-        ve.wait_ge(S["hv%d" % s], 2)
-        ve.wait_ge(S["hs%d" % s], 2)
+        ve.wait_ge(S["hv%d" % s], len(VE[s]))
+        ve.wait_ge(S["hs%d" % s], 4 - len(VE[s]))
         ve.quantize_mx(hq[:, 0:n], hp[:, 0:n], h[:, 0:4 * n]).then_inc(S["hq%d" % s], 1)
         te.wait_ge(S["hq%d" % s], 1)
         te.matmul_mx(T.zp[:, 2048 * s:2048 * s + n], T["wq%d" % e][:, 512:640], T["wp%d" % e][:, 512:640], hq[:, 0:n], hp[:, 0:n], True, True).then_inc(S["p%d" % s], 1)
+    parts = []
+    for j, c in q["land"]:
+        if parts and parts[-1][1] == c:
+            parts[-1] = (parts[-1][0], c + w[j][k])
+        else:
+            parts.append((c, c + w[j][k]))
+    g.wait_ge(S.lg, 16 * cnt)
+    for c, e in parts:
+        g.partition_broadcast(T.gw[:, c:e], T.gr[0:1, c:e], 128).then_inc(S.gb, 1)
+    ve.wait_ge(S.gb, len(parts))
+
+    def gated(out, src, c, m, sem):
+        ve.tensor_tensor(out, src, T.gw[:, c:c + m], AluOpType.mult).then_inc(sem, 1)
     far = [t for t in q["land"] if t[0] != rank]
     own = [t for t in q["land"] if t[0] == rank]
-    a, b = min(c for j, c in far), max(c + w[j][k] for j, c in far)
-    sc.wait_ge(S.p0, 1)
-    sc.activation(T.pr[:, a:b], T.zp[:, a:b], ActivationFunctionType.Copy).then_inc(S.es, 1)
+    ve.wait_ge(S.p0, 1)
+    nes = 0
+    for c, e in parts:
+        a, b = max(c, min(c for j, c in far)), min(e, max(c + w[j][k] for j, c in far))
+        if b > a:
+            gated(T.pr[:, a:b], T.zp[:, a:b], a, b - a, S.es)
+            nes += 1
     for j, c in own:
         o = P["pos"][j][k]
-        sc.activation(T.yl[:, o:o + w[j][k]], T.zp[:, c:c + w[j][k]], ActivationFunctionType.Copy).then_inc(S.es, 1)
-    ve.wait_ge(S.es, 1 + len(own))
+        gated(T.yl[:, o:o + w[j][k]], T.zp[:, c:c + w[j][k]], c, w[j][k], S.es)
+        nes += 1
+    ve.wait_ge(S.es, nes)
     ve.wait_ge(S.p1, 1)
-    g.wait_ge(S.es, 1 + len(own))
+    g.wait_ge(S.es, nes)
     for i, (j, c) in enumerate(far + own):
         o, cnt = P["pos"][j][k], 0
         for r, m, e in P["runs"](j, k):
             if e == order[1]:
                 out = T.yl[:, o + r:o + r + m] if j == rank else T.pr[:, c + r:c + r + m]
-                ve.tensor_copy(out, T.zp[:, 2048 + c + r:2048 + c + r + m]).then_inc(S["ev%d" % i], 1)
+                gated(out, T.zp[:, 2048 + c + r:2048 + c + r + m], c + r, m, S["ev%d" % i])
                 cnt += 1
         if cnt:
             (ve if j == rank else g).wait_ge(S["ev%d" % i], cnt)
@@ -337,28 +391,26 @@ def compute_side(g, core, rank, T, P, push, topo):
 
 def combine_side(g, rank, T, P, topo):
     S, v, k0, pair, cores = T.sem, g.vector, rank // 2, P["pair"][rank], P["cores"]
-    off = [sum(pair[:i]) for i in range(NK)]
-    v.wait_ge(S.gb, 1)
-    have, nm, nadd = [0] * NK, 0, 0
-    for k in [k0] + [k for k in range(NK) if k != k0]:
-        if k != k0 and P["width"][rank][k]:
-            v.wait_ge(S["y%d" % k], len(bits(topo.mask(P["dest"][rank, k], cores[rank]))))
-        a, done = P["pos"][rank][k], []
-        for second, pk in ((1, (k - 1) % NK), (0, k)):
-            n, o = pair[pk], off[pk]
-            have[pk] += 1
-            if n:
-                t = T.t2 if second else T.t1
-                v.tensor_tensor(t[:, o:o + n], T.yl[:, a:a + n], T.gb[:, NC * second + o:NC * second + o + n], AluOpType.mult).then_inc(S.m, 1)
-                nm += 1
-                a += n
-                if have[pk] == 2:
-                    done.append((o, n))
-        if done:
-            v.wait_ge(S.m, nm)
-        for o, n in done:
-            v.tensor_tensor(T.yo[:, o:o + n], T.t1[:, o:o + n], T.t2[:, o:o + n], AluOpType.add).then_inc(S.yd, 1)
-            nadd += 1
+    width, pos = P["width"][rank], P["pos"][rank]
+
+    def due(k):
+        if k == k0 or not width[k]:
+            return -1
+        q = P["comp"][P["dest"][rank, k]]
+        return q["from"].index(rank) + q["n"] / 300
+    seen, nadd = [k0], 0
+    for p in sorted(range(NK), key=lambda p: max(due(p), due((p + 1) % NK))):
+        n, nx = pair[p], (p + 1) % NK
+        if not n:
+            continue
+        for k in sorted((p, nx), key=due):
+            if k not in seen:
+                v.wait_ge(S["y%d" % k], len(bits(topo.mask(P["dest"][rank, k], cores[rank]))))
+                seen.append(k)
+        a, b, o = pos[p] + pair[p - 1], pos[nx], sum(pair[:p])
+        v.tensor_tensor(T.yo[:, o:o + n], T.yl[:, a:a + n], T.yl[:, b:b + n], AluOpType.add).then_inc(S.yd, 1)
+        nadd += 1
+    assert all(k in seen for k in range(NK) if width[k])
     g.sync.wait_ge(S.yd, nadd)
     g.sync.dma_start(T.y[:], T.yo[:]).then_inc(S.st, 16)
     g.sync.wait_ge(S.st, 16)

@@ -2,34 +2,32 @@ from concourse.bass import DstId, RemoteDMATransfer
 from concourse.mybir import dt, AluOpType, ActivationFunctionType
 
 N, NC, ALL = 12, 256, 256
-NK = N // 2
+S2 = 2
+SLOTS = 9
 GAIN = 0.019
 BYTES = dt.uint8
 Q8, U8, BF, F4 = "float8_e4m3fn_x4", "uint8", "bfloat16", "float32"
-VE = ((0, 2), (1, 3))
 SCRATCH = {
     "xt": ("sbuf", [128, 4 * 384], BF),
     "xq": ("sbuf", [128, 384], Q8), "xp": ("sbuf", [128, 384], U8),
     "rq": ("sbuf", [128, 384], Q8), "rp": ("sbuf", [128, 384], U8),
-    "lq": ("sbuf", [128, 640], Q8), "lp": ("sbuf", [128, 640], U8),
+    "lq": ("sbuf", [128, 768], Q8), "lp": ("sbuf", [128, 768], U8),
     "w1t": ("sbuf", [128, 2048], BF), "w2t": ("sbuf", [128, 512], BF),
-    "wq0": ("sbuf", [128, 640], Q8), "wp0": ("sbuf", [128, 640], U8),
-    "wq1": ("sbuf", [128, 640], Q8), "wp1": ("sbuf", [128, 640], U8),
-    "h0": ("sbuf", [128, 2048], BF), "h1": ("sbuf", [128, 2048], BF),
-    "hq0": ("sbuf", [128, 512], Q8), "hp0": ("sbuf", [128, 512], U8),
-    "hq1": ("sbuf", [128, 512], Q8), "hp1": ("sbuf", [128, 512], U8),
+    "wq": ("sbuf", [128, 640], Q8), "wp": ("sbuf", [128, 640], U8),
+    "h0": ("sbuf", [128, 2048], BF), "hq0": ("sbuf", [128, 512], Q8), "hp0": ("sbuf", [128, 512], U8),
+    "h1": ("sbuf", [128, 2048], BF), "hq1": ("sbuf", [128, 512], Q8), "hp1": ("sbuf", [128, 512], U8),
     "zp": ("psum", [128, 4096], F4),
     "pr": ("sbuf", [128, 512], F4),
     "yl": ("sbuf", [128, 512], F4),
     "yo": ("sbuf", [128, 256], F4),
     "gd": ("dram", [128, 4], BF), "gf": ("dram", [128, 4], BF),
-    "gi0": ("dram", [128, 4], BF), "gi1": ("dram", [128, 4], BF), "gi2": ("dram", [128, 4], BF),
     "gr": ("sbuf", [128, 512], BF), "gw": ("sbuf", [128, 512], BF),
 }
-SEMAPHORES = (["lx", "lw1", "lw2", "ld", "lg", "gb", "gf", "ga", "qx", "qo", "qw", "rc", "rp", "xa", "w0", "w1", "ls", "yd", "st", "es"]
-              + ["z%d%d" % (s, i) for s in range(2) for i in range(4)]
-              + [n + str(s) for n in ("hv", "hs", "hq", "p") for s in range(2)]
-              + ["ev%d" % k for k in range(4)] + ["y%d" % k for k in range(NK)])
+for _i in range(SLOTS):
+    SCRATCH["gi%d" % _i] = ("dram", [128, 4], BF)
+SEMAPHORES = (["lx", "lw1", "lw2", "ld", "lg", "gb", "gf", "ga", "qx", "qo", "qw", "rc", "rp",
+               "xa0", "xa1", "w", "ls", "yd", "st", "hv0", "hs0", "hq0", "p0", "hv1", "hs1", "hq1", "p1", "ev0", "ev1", "ev2"]
+              + ["z%d%d" % (b, i) for b in range(2) for i in range(4)] + ["y%d" % k for k in range(N)])
 CACHE = {}
 
 
@@ -49,6 +47,7 @@ def plan(T, topo):
     if CACHE:
         return CACHE
     cores, cnt = list(T.cores), T.tables["CNT"]
+    off = [[sum(c[:e]) for e in range(N + 1)] for c in cnt]
 
     def same_chip(a, b):
         return (topo.host(a), topo.chip(a)) == (topo.host(b), topo.chip(b))
@@ -57,133 +56,169 @@ def plan(T, topo):
         return all(topo.may_write(c, d) for d in cores if d != c)
 
     def helpers(c):
-        return [d for d in range(ALL) if same_chip(c, d) and d not in cores and topo.die(d) == topo.die(c) and owner(d)]
+        hs = [d for d in range(ALL) if same_chip(c, d) and d not in cores and topo.die(d) == topo.die(c)]
+        return sorted(hs, key=lambda d: (not owner(d), d))
 
-    pair = [[c[2 * k] + c[2 * k + 1] for k in range(NK)] for c in cnt]
-    wrap = [p[-1] for p in pair]
+    start, width, runs, need, wrap = [], [], [], [], []
+    for c, o in zip(cnt, off):
+        both = [e for e in range(S2) if c[e] and c[e - S2]]
+        wr = sum(c[both[0] - S2:]) if both else 0
+        st, wd, rn = [], [], []
+        for e in range(N):
+            f = (e - S2) % N
+            pf = wr + o[f] - (NC if e in both else 0)
+            s = pf if c[f] else wr + o[e]
+            end = wr + o[e + 1] if c[e] else s + c[f]
+            st.append(s)
+            wd.append(end - s)
+            rn.append([(w, r, p, c[r]) for w, r, p in ((1, f, 0), (0, e, end - s - c[e])) if c[r]])
+        start.append(st)
+        width.append(wd)
+        runs.append(rn)
+        need.append([c[e - S2] + c[e] for e in range(N)])
+        wrap.append(wr)
     tot = [NC + w for w in wrap]
-    start = [[sum(([wrap[j]] + pair[j])[:k]) for k in range(NK)] for j in range(N)]
-    width = [[pair[j][k - 1] + pair[j][k] for k in range(NK)] for j in range(N)]
-    pos = [[sum(width[j][:k]) for k in range(NK)] for j in range(N)]
+    pos = [[sum(need[j][:e]) for e in range(N)] for j in range(N)]
 
-    comp, dest = {}, {}
-    entry = {(k, x): 0 for k in range(NK) for x in {topo.die(c) for c in cores}}
-    for k in range(NK):
-        a, b = cores[2 * k], cores[2 * k + 1]
-        cc = [a, helpers(a)[0], b, helpers(b)[0]]
-        others = sorted([j for j in range(N) if j // 2 != k and width[j][k]], key=lambda j: -width[j][k])
-        load = {a: width[2 * k][k], b: width[2 * k + 1][k], cc[1]: 0, cc[3]: 0}
-        room = {a: 2, b: 2, cc[1]: 3, cc[3]: 3}
-        best, pick = [10 ** 6, None], {}
+    comp, dest, team = {}, {}, {}
+    dies = sorted({topo.die(c) for c in cores})
+    entry = {(k, x): 0 for k in range(N // 2) for x in dies}
+    for e in range(N):
+        c = cores[e]
+        team[e] = [c] + [helpers(d)[0] for d in cores if same_chip(c, d) and topo.die(d) != topo.die(c)]
+        if 2 * sum(topo.may_write(c, d) for d in cores if d != c) < N:
+            team[e].append(helpers(c)[1])
+    for turn in range(3):
+        for e in range(N):
+            cc = team[e]
+            others = sorted([j for j in range(N) if j != e and need[j][e]], key=lambda j: -width[j][e])
+            load, num = {d: 0 for d in cc}, {d: 0 for d in cc}
+            load[cores[e]] = width[e][e]
+            best, pick = [10 ** 9, None], {}
 
-        def search(i):
-            cost = max(load.values()) + max(entry.values())
-            if cost >= best[0]:
-                return
-            if i == len(others):
-                best[0], best[1] = cost, dict(pick)
-                return
-            j = others[i]
+            def count(j, d, s):
+                load[d] += s * width[j][e]
+                num[d] += s
+                if not same_chip(d, cores[j]):
+                    entry[j // 2, topo.die(d)] += s * need[j][e]
+            if turn:
+                for j in others:
+                    entry[j // 2, topo.die(dest[j, e])] -= 0 if same_chip(cores[e], cores[j]) else need[j][e]
+
+            def search(i):
+                if max(load[d] + 16 * num[d] for d in cc) >= best[0]:
+                    return
+                if i == len(others):
+                    cost = (max(load[d] + 16 * num[d] for d in cc)
+                            + sum(abs(entry[k, dies[0]] - entry[k, dies[1]]) for k in range(N // 2)) // 4)
+                    if cost < best[0] and all(128 <= load[d] <= 512 for d in cc[1:]):
+                        best[0], best[1] = cost, dict(pick)
+                    return
+                j = others[i]
+                for d in cc:
+                    if num[d] < SLOTS and topo.may_write(d, cores[j]):
+                        pick[j] = d
+                        count(j, d, 1)
+                        search(i + 1)
+                        count(j, d, -1)
+            search(0)
             for d in cc:
-                if room[d] and topo.may_write(d, cores[j]) and (d not in cores or topo.may_write(cores[j], d)):
-                    room[d] -= 1
-                    load[d] += width[j][k]
-                    entry[j // 2, topo.die(d)] += width[j][k]
-                    pick[j] = d
-                    search(i + 1)
-                    room[d] += 1
-                    load[d] -= width[j][k]
-                    entry[j // 2, topo.die(d)] -= width[j][k]
-        search(0)
-        for d in cc:
-            lead = a if topo.die(d) == topo.die(a) else b
-            comp[d] = {"k": k, "own": cores.index(d) if d in cores else None, "lead": cores.index(lead) % 2,
-                       "from": [j for j in sorted(others) if best[1][j] == d]}
-        for j in others:
-            dest[j, k] = best[1][j]
-            entry[j // 2, topo.die(best[1][j])] += width[j][k]
+                comp[d] = {"e": e, "own": e if d == cores[e] else None, "from": [j for j in others if best[1][j] == d]}
+            for j in others:
+                dest[j, e] = best[1][j]
+                entry[j // 2, topo.die(dest[j, e])] += 0 if same_chip(cores[e], cores[j]) else need[j][e]
 
-    relay, direct, via = {}, {}, {}
+    via, relay = {}, {}
     for j in range(N):
         c = cores[j]
-        away = [k for k in range(NK) if k != j // 2 and width[j][k]]
-        plane = [k for k in away if topo.same_plane(c, cores[2 * k])]
-        cross = [k for k in away if k not in plane]
-        hl = helpers(c)
-        relay[j] = [(hl[0], k) for k in cross[:2]] if owner(c) else [(hl[i % len(hl)], k) for i, k in enumerate(cross)]
-        direct[j] = [k for k in plane + cross if k not in [kk for h, kk in relay[j]]]
-        for k in direct[j]:
-            via[j, k] = c
-        for h, k in relay[j]:
-            via[j, k] = h
-    gvia = {(j, k): cores[j] if dest[j, k] in cores else via[j, k] for j, k in via}
+        hs = helpers(c)[:3]
+        away = [e for e in range(N) if (j, e) in dest]
+        near = [e for e in away if same_chip(dest[j, e], c)]
+        cross = [e for e in away if e not in near and not all(topo.may_write(s, dest[j, e]) for s in [c] + hs)]
+        own = [s for s in hs + [c] if all(topo.may_write(s, dest[j, e]) for e in cross)]
+        num = {s: 0 for s in [c] + hs}
+        for e in near:
+            via[j, e] = c
+            num[c] += 0.5
+        for i, e in enumerate(cross):
+            s = own[i * len(own) // len(cross)]
+            via[j, e] = s
+            num[s] += 1
+        rest, order = [e for e in away if (j, e) not in via], [s for s in hs if s not in own] + [c] + [s for s in own if s != c]
+        level = 1
+        while sum(max(0, int(level - num[s])) for s in order) < len(rest):
+            level += 0.5
+        for s in order:
+            while rest and num[s] + 1 <= level:
+                via[j, rest.pop(0)] = s
+                num[s] += 1
+        assert not rest
+        relay[j] = [h for h in hs if num[h]]
+        relay[j].sort(key=lambda h: -num[h])
 
     send = {}
     for d, q in comp.items():
-        k, own, col, land = q["k"], q["own"], 0, []
+        e, own, col, land = q["e"], q["own"], 0, []
         q["lo"] = 0
         if own is not None:
-            w, s = width[own][k], start[own][k]
+            w, s = width[own][e], start[own][e]
             m = max(128, up16(w))
             ahead = s + w >= m
             if ahead:
                 q["fill"], q["lo"], col = (0, s + w - m, m), m - w, m
-                land.append((own, m - w))
+                if w:
+                    land.append((own, m - w))
         for i, j in enumerate(q["from"]):
-            s, n, lead = start[j][k], width[j][k], 0
+            s, n, lead = start[j][e], width[j][e], 0
             if own is not None and not ahead and i == len(q["from"]) - 1 and (col + n) % 16:
                 lead = 0 if s + n + 8 <= tot[j] else 8
                 s, n = s - lead, n + 8
-            send[j, k] = (s, n, col)
+            send[j, e] = (s, n, col)
             land.append((j, col + lead))
             col += n
         if own is not None and not ahead:
-            s, n = start[own][k], width[own][k]
+            s, n = start[own][e], width[own][e]
             q["fill"] = (col, s, max(128, up16(n)))
             assert col % 16 == 0 and s + q["fill"][2] <= tot[own]
-            land.append((own, col))
-            col += n
-        q["n"] = col - q["lo"]
-        assert 128 <= q["n"] <= 512
-        q["land"] = [(j, c - q["lo"]) for j, c in land]
+            if n:
+                land.append((own, col))
+            col = max(128, col + n)
+        q["lo"] = min(q["lo"], max(0, col - 128))
+        q["n"] = n = col - q["lo"]
+        assert 128 <= n <= 512
+        q["land"] = land = [(j, c - q["lo"]) for j, c in land]
+        q["ans"] = {j: sum(need[i][e] for i, _ in land[:k]) for k, (j, _) in enumerate(land)}
+        mid = min([c for j, c in land if c >= 128] or [n], key=lambda c: abs(c - n // 2))
+        two = n - mid >= 48
+        q["batches"] = [(0, mid), (min(mid, n - 128), max(128, n - mid))] if two else [(0, n)]
+        q["batch"] = {j: int(two and c >= mid) for j, c in land}
 
     span, skip = {}, {}
     for j in range(N):
-        hs = [h for i, (h, k) in enumerate(relay[j]) if h not in [x for x, y in relay[j][:i]]]
-        lo = {h: min(send[j, k][0] for x, k in relay[j] if x == h) for h in hs}
-        hi = {h: max(send[j, k][0] + send[j, k][1] for x, k in relay[j] if x == h) for h in hs}
-        w = max(hi[h] - lo[h] for h in hs)
-        span[j] = [(h, min(lo[h], tot[j] - w), w) for h in hs]
-        for h, s, w in span[j]:
-            for x, k in relay[j]:
-                if x == h:
-                    skip[j, k] = send[j, k][0] - s
+        span[j] = []
+        for h in relay[j]:
+            es = [e for e in range(N) if via.get((j, e)) == h]
+            lo = min(send[j, e][0] for e in es)
+            hi = max(send[j, e][0] + send[j, e][1] for e in es)
+            span[j].append((h, lo, hi))
+            for e in es:
+                skip[j, e] = send[j, e][0] - lo
 
-    def runs(j, k):
-        out, c = [], 0
-        for i, r in enumerate((2 * k - 2, 2 * k - 1, 2 * k, 2 * k + 1)):
-            n = cnt[j][r % N]
-            if n:
-                out.append((c, n, i % 2))
-            c += n
-        return out
-
-    CACHE.update(cores=cores, pair=pair, wrap=wrap, tot=tot, start=start, width=width, pos=pos, runs=runs, comp=comp, dest=dest,
-                 relay=relay, direct=direct, via=via, gvia=gvia, send=send, span=span, skip=skip)
+    CACHE.update(cores=cores, cnt=cnt, off=off, need=need, runs=runs, pos=pos, tot=tot, wrap=wrap, comp=comp, dest=dest, via=via,
+                 send=send, span=span, skip=skip, entry=entry)
     return CACHE
 
 
-def weight_dests(core, P, topo):
-    k = P["comp"][core]["k"]
-    ds = [d for d, q in P["comp"].items() if q["k"] == k and d != core]
-    return [d for d in ds if topo.die(d) == topo.die(core)], [d for d in ds if topo.die(d) != topo.die(core)]
+def weight_dests(core, P):
+    e = P["comp"][core]["e"]
+    return [d for d, q in P["comp"].items() if q["e"] == e and d != core]
 
 
 def engine_halves(core, P, topo):
     out = [d for d in P["cores"] if d != core and topo.may_write(core, d)
            and (topo.host(d), topo.chip(d)) != (topo.host(core), topo.chip(core))][0]
     lo = bits(topo.mask(core, out))
-    return lo, [b for b in bits(topo.mask(core, weight_dests(core, P, topo)[0][0])) if b not in lo]
+    return lo, [b for b in bits(topo.mask(core, weight_dests(core, P)[0])) if b not in lo]
 
 
 def rank_program(g, core, T, topo):
@@ -209,7 +244,7 @@ def rank_program(g, core, T, topo):
 
     if rank is not None:
         send_side(g, core, rank, T, P, push, fused, topo)
-    helping = [(j, k) for (j, k), h in P["via"].items() if h == core and j != rank]
+    helping = [(j, e) for (j, e), h in P["via"].items() if h == core and j != rank]
     if helping:
         relay_side(g, core, T, P, helping, push, fused, topo)
     if core in P["comp"]:
@@ -221,16 +256,19 @@ def rank_program(g, core, T, topo):
 
 
 def gate_slots(T, P, j, core):
-    out = []
-    for k in range(NK):
-        if P["gvia"].get((j, k)) == core:
-            d = P["dest"][j, k]
-            out.append((d, T["gi%d" % P["comp"][d]["from"].index(j)][:]))
-    return out
+    return [(P["dest"][j, e], T["gi%d" % P["comp"][P["dest"][j, e]]["from"].index(j)][:])
+            for e in range(N) if P["via"].get((j, e)) == core]
+
+
+def window_to(T, P, j, e, push, q, p, a):
+    (_, w, c), d = P["send"][j, e], P["dest"][j, e]
+    sem = T.sem["xa%d" % P["comp"][d]["batch"][j]]
+    push(d, codes(T.lq[:, c:c + w]), codes(q[:, a:a + w]), sem)
+    push(d, T.lp[:, c:c + w], p[:, a:a + w], sem)
 
 
 def send_side(g, core, rank, T, P, push, fused, topo):
-    S, tot, wrap, par = T.sem, P["tot"][rank], P["wrap"][rank], rank % 2
+    S, tot, wrap, v = T.sem, P["tot"][rank], P["wrap"][rank], g.vector
     g.scalar.dma_start(T.gd[:], T.gt[:]).then_inc(S.ld, 16)
     g.sync.dma_start(T.xt[:, 4 * wrap:4 * tot], T.x[:]).then_inc(S.lx, 16)
     if wrap:
@@ -238,68 +276,51 @@ def send_side(g, core, rank, T, P, push, fused, topo):
     g.sync.dma_start(T.w1t[:], T.w1[:]).then_inc(S.lw1, 16)
     g.sync.dma_start(T.w2t[:], T.w2[:]).then_inc(S.lw2, 16)
 
-    v = g.vector
     v.wait_ge(S.lx, 32 if wrap else 16)
     v.quantize_mx(T.xq[:, 0:tot], T.xp[:, 0:tot], T.xt[:, 0:4 * tot]).then_inc(S.qx, 1)
     p, s, m = P["comp"][core]["fill"]
     v.quantize_mx(T.lq[:, p:p + m], T.lp[:, p:p + m], T.xt[:, 4 * s:4 * (s + m)]).then_inc(S.qo, 1)
-    wq, wp = T["wq%d" % par], T["wp%d" % par]
     v.wait_ge(S.lw1, 16)
-    v.quantize_mx(wq[:, 0:512], wp[:, 0:512], T.w1t[:]).then_inc(S.qw, 1)
+    v.quantize_mx(T.wq[:, 0:512], T.wp[:, 0:512], T.w1t[:]).then_inc(S.qw, 1)
     v.wait_ge(S.lw2, 16)
-    v.quantize_mx(wq[:, 512:640], wp[:, 512:640], T.w2t[:]).then_inc(S.qw, 1)
+    v.quantize_mx(T.wq[:, 512:640], T.wp[:, 512:640], T.w2t[:]).then_inc(S.qw, 1)
 
     lo, hi = engine_halves(core, P, topo)
-    direct, sp = P["direct"][rank], P["span"][rank]
-    near, far = [(h, T.gf[:]) for h, s, w in sp if gate_slots(T, P, rank, h)], gate_slots(T, P, rank, core)
+    sp = P["span"][rank]
     g.wait_ge(S.ld, 16)
+    far, near = gate_slots(T, P, rank, core), [(h, T.gf[:]) for h, a, b in sp]
     fused(([(far, T.gd[:], S.ga, lo)] if far else []) + ([(near, T.gd[:], S.gf, hi)] if near else []))
     g.wait_ge(S.qx, 1)
-    eng = bits(topo.mask(core, sp[0][0]))
-    per = len(eng) // len(sp)
-    fused([([(h, codes(T.rq[:, 0:w]))], codes(T.xq[:, s:s + w]), S.rc, eng[i * per:i * per + per]) for i, (h, s, w) in enumerate(sp)])
-    fused([([(h, T.rp[:, 0:w])], T.xp[:, s:s + w], S.rp, eng[i * per:i * per + per]) for i, (h, s, w) in enumerate(sp)])
-
-    def windows(ks):
-        for k in ks:
-            s, w, c = P["send"][rank, k]
-            d = P["dest"][rank, k]
-            push(d, codes(T.lq[:, c:c + w]), codes(T.xq[:, s:s + w]), S.xa)
-            push(d, T.lp[:, c:c + w], T.xp[:, s:s + w], S.xa)
-    windows(direct[:1])
+    for h, a, b in sp:
+        push(h, codes(T.rq[:, 0:b - a]), codes(T.xq[:, a:b]), S.rc)
+        push(h, T.rp[:, 0:b - a], T.xp[:, a:b], S.rp)
+    for e in range(N):
+        if P["via"].get((rank, e)) == core:
+            window_to(T, P, rank, e, push, T.xq, T.xp, P["send"][rank, e][0])
     g.wait_ge(S.qw, 2)
-    near, far = weight_dests(core, P, topo)
-    sem = S["w%d" % par]
-    fused([([(d, codes(wq[:])) for d in far], codes(wq[:]), sem, hi), ([(d, codes(wq[:])) for d in near], codes(wq[:]), sem, lo)])
-    fused([([(d, wp[:]) for d in far], wp[:], sem, hi), ([(d, wp[:]) for d in near], wp[:], sem, lo)])
-    windows(direct[1:])
+    ds = weight_dests(core, P)
+    fused([([(d, codes(T.wq[:]))], codes(T.wq[:]), S.w, eng) for d, eng in zip(ds, (hi, lo))])
+    fused([([(d, T.wp[:])], T.wp[:], S.w, eng) for d, eng in zip(ds, (lo, hi))])
 
 
 def relay_side(g, core, T, P, helping, push, fused, topo):
     S, j = T.sem, helping[0][0]
     src = P["cores"][j]
-    n = len(bits(topo.mask(src, core))) // len(P["span"][j])
-    slots = gate_slots(T, P, j, core)
-    if slots:
-        g.wait_ge(S.gf, len(engine_halves(src, P, topo)[1]))
-        fused([(slots, T.gf[:], S.ga, bits(topo.mask(core, slots[0][0])))])
+    lo, hi = engine_halves(src, P, topo)
+    n = len(bits(topo.mask(src, core)))
+    g.wait_ge(S.gf, len(hi))
+    fused([(gate_slots(T, P, j, core), T.gf[:], S.ga, lo)])
     g.wait_ge(S.rc, n)
-    for j, k in helping:
-        a, (_, w, c), d = P["skip"][j, k], P["send"][j, k], P["dest"][j, k]
-        push(d, codes(T.lq[:, c:c + w]), codes(T.rq[:, a:a + w]), S.xa)
     g.wait_ge(S.rp, n)
-    for j, k in helping:
-        a, (_, w, c), d = P["skip"][j, k], P["send"][j, k], P["dest"][j, k]
-        push(d, T.lp[:, c:c + w], T.rp[:, a:a + w], S.xa)
+    for j, e in helping:
+        window_to(T, P, j, e, push, T.rq, T.rp, P["skip"][j, e])
 
 
 def compute_side(g, core, rank, T, P, push, topo):
-    S, q, cores, w = T.sem, P["comp"][core], P["cores"], P["width"]
-    k, n, lo = q["k"], q["n"], q["lo"]
-    order = (q["lead"], 1 - q["lead"])
+    S, q, cores = T.sem, P["comp"][core], P["cores"]
+    e, lo, bat, ans = q["e"], q["lo"], q["batches"], q["ans"]
     te, ve, sc = g.tensor, g.vector, g.scalar
-    arr = sum(2 * len(bits(topo.mask(P["via"][j, k], core))) for j in q["from"])
-    cnt = 0
+    num = 0
     for j, c in sorted(q["land"], key=lambda t: t[0] != rank):
         if j == rank:
             src = T.gd
@@ -307,110 +328,98 @@ def compute_side(g, core, rank, T, P, push, topo):
         else:
             src = T["gi%d" % q["from"].index(j)]
             if j == q["from"][0]:
-                g.sync.wait_ge(S.ga, sum(len(bits(topo.mask(P["gvia"][i, k], core))) for i in q["from"]))
-        for which, pk in ((1, (k - 1) % NK), (0, k)):
-            m = P["pair"][j][pk]
-            if m:
-                r = (NC * which + sum(P["pair"][j][:pk])) // 4
-                g.sync.dma_start(T.gr[0:1, c:c + m], src[r:r + m // 4, :]).then_inc(S.lg, 16)
-                c += m
-                cnt += 1
-    x, xs = T.lq[:, lo:lo + n], T.lp[:, lo:lo + n]
-    for s, e in enumerate(order):
-        wq, wp = T["wq%d" % e], T["wp%d" % e]
-        src = cores[2 * k + e]
-        if src == core:
-            te.wait_ge(S.qw, 2)
-        else:
-            a, b = engine_halves(src, P, topo)
-            te.wait_ge(S["w%d" % e], 2 * len(a if core in weight_dests(src, P, topo)[0] else b))
-        if s == 0:
-            if rank is not None:
-                te.wait_ge(S.qo, 1)
-            te.wait_ge(S.xa, arr)
+                g.sync.wait_ge(S.ga, sum(len(engine_halves(cores[i], P, topo)[0]) for i in q["from"]))
+        k = ans[j]
+        for which, r, p, m in P["runs"][j][e]:
+            row = (NC * which + P["off"][j][r]) // 4
+            g.sync.dma_start(T.gr[0:1, k:k + m], src[row:row + m // 4, :]).then_inc(S.lg, 16)
+            k += m
+            num += 1
+    if rank is not None:
+        te.wait_ge(S.qw, 2)
+        te.wait_ge(S.qo, 1)
+    else:
+        te.wait_ge(S.w, sum(len(b) for b in engine_halves(cores[e], P, topo)))
+    for b, (a, m) in enumerate(bat):
+        arr = sum(2 * len(bits(topo.mask(P["via"][j, e], core))) for j in q["from"] if q["batch"][j] == b)
+        if arr:
+            te.wait_ge(S["xa%d" % b], arr)
+        x, xs = T.lq[:, lo + a:lo + a + m], T.lp[:, lo + a:lo + a + m]
         for i in range(4):
-            o = 512 * (4 * s + i)
-            te.matmul_mx(T.zp[:, o:o + n], wq[:, 128 * i:128 * i + 128], wp[:, 128 * i:128 * i + 128], x, xs, True, True).then_inc(S["z%d%d" % (s, i)], 1)
-    for s, e in enumerate(order):
-        h, hq, hp = T["h%d" % s], T["hq%d" % s], T["hp%d" % s]
+            o = 512 * (4 * b + i)
+            te.matmul_mx(T.zp[:, o:o + m], T.wq[:, 128 * i:128 * i + 128], T.wp[:, 128 * i:128 * i + 128], x, xs, True, True).then_inc(S["z%d%d" % (b, i)], 1)
+    for b, (a, m) in enumerate(bat):
+        h, hq, hp = T["h%d" % b], T["hq%d" % b], T["hp%d" % b]
         for i in range(4):
-            o = 512 * (4 * s + i)
-            out, z, sem = h[:, i:4 * n:4], T.zp[:, o:o + n], S["z%d%d" % (s, i)]
-            if i in VE[s]:
+            o = 512 * (4 * b + i)
+            out, z, sem = h[:, i:4 * m:4], T.zp[:, o:o + m], S["z%d%d" % (b, i)]
+            if i % 2 == b:
                 ve.wait_ge(sem, 1)
-                ve.tensor_scalar(out, z, 0.0, GAIN, AluOpType.max, AluOpType.mult).then_inc(S["hv%d" % s], 1)
+                ve.tensor_scalar(out, z, 0.0, GAIN, AluOpType.max, AluOpType.mult).then_inc(S["hv%d" % b], 1)
             else:
                 sc.wait_ge(sem, 1)
-                sc.activation(out, z, ActivationFunctionType.Relu, scale=GAIN).then_inc(S["hs%d" % s], 1)
-        ve.wait_ge(S["hv%d" % s], len(VE[s]))
-        ve.wait_ge(S["hs%d" % s], 4 - len(VE[s]))
-        ve.quantize_mx(hq[:, 0:n], hp[:, 0:n], h[:, 0:4 * n]).then_inc(S["hq%d" % s], 1)
-        te.wait_ge(S["hq%d" % s], 1)
-        te.matmul_mx(T.zp[:, 2048 * s:2048 * s + n], T["wq%d" % e][:, 512:640], T["wp%d" % e][:, 512:640], hq[:, 0:n], hp[:, 0:n], True, True).then_inc(S["p%d" % s], 1)
-    parts = []
-    for j, c in q["land"]:
-        if parts and parts[-1][1] == c:
-            parts[-1] = (parts[-1][0], c + w[j][k])
-        else:
-            parts.append((c, c + w[j][k]))
-    g.wait_ge(S.lg, 16 * cnt)
-    for c, e in parts:
-        g.partition_broadcast(T.gw[:, c:e], T.gr[0:1, c:e], 128).then_inc(S.gb, 1)
-    ve.wait_ge(S.gb, len(parts))
-
-    def gated(out, src, c, m, sem):
-        ve.tensor_tensor(out, src, T.gw[:, c:c + m], AluOpType.mult).then_inc(sem, 1)
-    far = [t for t in q["land"] if t[0] != rank]
-    own = [t for t in q["land"] if t[0] == rank]
-    ve.wait_ge(S.p0, 1)
-    nes = 0
-    for c, e in parts:
-        a, b = max(c, min(c for j, c in far)), min(e, max(c + w[j][k] for j, c in far))
-        if b > a:
-            gated(T.pr[:, a:b], T.zp[:, a:b], a, b - a, S.es)
-            nes += 1
-    for j, c in own:
-        o = P["pos"][j][k]
-        gated(T.yl[:, o:o + w[j][k]], T.zp[:, c:c + w[j][k]], c, w[j][k], S.es)
-        nes += 1
-    ve.wait_ge(S.es, nes)
-    ve.wait_ge(S.p1, 1)
-    g.wait_ge(S.es, nes)
-    for i, (j, c) in enumerate(far + own):
-        o, cnt = P["pos"][j][k], 0
-        for r, m, e in P["runs"](j, k):
-            if e == order[1]:
-                out = T.yl[:, o + r:o + r + m] if j == rank else T.pr[:, c + r:c + r + m]
-                gated(out, T.zp[:, 2048 + c + r:2048 + c + r + m], c + r, m, S["ev%d" % i])
-                cnt += 1
-        if cnt:
-            (ve if j == rank else g).wait_ge(S["ev%d" % i], cnt)
-        if j != rank:
-            push(cores[j], T.yl[:, o:o + w[j][k]], T.pr[:, c:c + w[j][k]], S["y%d" % k])
+                sc.activation(out, z, ActivationFunctionType.Relu, scale=GAIN).then_inc(S["hs%d" % b], 1)
+        ve.wait_ge(S["hv%d" % b], 2)
+        ve.wait_ge(S["hs%d" % b], 2)
+        ve.quantize_mx(hq[:, 0:m], hp[:, 0:m], h[:, 0:4 * m]).then_inc(S["hq%d" % b], 1)
+        te.wait_ge(S["hq%d" % b], 1)
+        te.matmul_mx(T.zp[:, 2048 * b:2048 * b + m], T.wq[:, 512:640], T.wp[:, 512:640], hq[:, 0:m], hp[:, 0:m], True, True).then_inc(S["p%d" % b], 1)
+    end = sum(P["need"][j][e] for j, c in q["land"])
+    g.wait_ge(S.lg, 16 * num)
+    g.partition_broadcast(T.gw[:, 0:end], T.gr[0:1, 0:end], 128).then_inc(S.gb, 1)
+    ve.wait_ge(S.gb, 1)
+    for b, (a, m) in enumerate(bat):
+        def gated(out, k, src, m):
+            o = 2048 * b + src - a
+            return ve.tensor_tensor(out, T.zp[:, o:o + m], T.gw[:, k:k + m], AluOpType.mult)
+        ve.wait_ge(S["p%d" % b], 1)
+        grp, calls = [t for t in q["land"] if t[0] != rank and q["batch"][t[0]] == b], []
+        for j, c in grp:
+            k = ans[j]
+            for _, r, p, m in P["runs"][j][e]:
+                if calls and calls[-1][0] + calls[-1][2] == k and calls[-1][1] + calls[-1][2] == c + p:
+                    calls[-1][2] += m
+                else:
+                    calls.append([k, c + p, m])
+                k += m
+        for k, src, m in calls:
+            gated(T.pr[:, k:k + m], k, src, m).then_inc(S["ev%d" % b], 1)
+        if grp:
+            g.wait_ge(S["ev%d" % b], len(calls))
+        for j, c in grp:
+            k, o, m = ans[j], P["pos"][j][e], P["need"][j][e]
+            push(cores[j], T.yl[:, o:o + m], T.pr[:, k:k + m], S["y%d" % e])
+        for j, c in q["land"]:
+            if j == rank and q["batch"][j] == b:
+                k, o = ans[j], P["pos"][j][e]
+                for _, r, p, m in P["runs"][j][e]:
+                    gated(T.yl[:, o:o + m], k, c + p, m).then_inc(S.ev2, 1)
+                    k, o = k + m, o + m
+                ve.wait_ge(S.ev2, len(P["runs"][j][e]))
 
 
 def combine_side(g, rank, T, P, topo):
-    S, v, k0, pair, cores = T.sem, g.vector, rank // 2, P["pair"][rank], P["cores"]
-    width, pos = P["width"][rank], P["pos"][rank]
+    S, v, cnt, off, cores = T.sem, g.vector, P["cnt"][rank], P["off"][rank], P["cores"]
+    need, pos = P["need"][rank], P["pos"][rank]
 
-    def due(k):
-        if k == k0 or not width[k]:
+    def due(e):
+        if e == rank or not need[e]:
             return -1
-        q = P["comp"][P["dest"][rank, k]]
-        return q["from"].index(rank) + q["n"] / 300
-    seen, nadd = [k0], 0
-    for p in sorted(range(NK), key=lambda p: max(due(p), due((p + 1) % NK))):
-        n, nx = pair[p], (p + 1) % NK
+        q = P["comp"][P["dest"][rank, e]]
+        return q["from"].index(rank) + q["n"] / 100
+    seen, nadd = [rank], 0
+    for r in sorted(range(N), key=lambda r: max(due(r), due((r + S2) % N))):
+        n, f = cnt[r], (r + S2) % N
         if not n:
             continue
-        for k in sorted((p, nx), key=due):
-            if k not in seen:
-                v.wait_ge(S["y%d" % k], len(bits(topo.mask(P["dest"][rank, k], cores[rank]))))
-                seen.append(k)
-        a, b, o = pos[p] + pair[p - 1], pos[nx], sum(pair[:p])
+        for e in sorted((r, f), key=due):
+            if e not in seen:
+                v.wait_ge(S["y%d" % e], len(bits(topo.mask(P["dest"][rank, e], cores[rank]))))
+                seen.append(e)
+        a, b, o = pos[r] + cnt[r - S2], pos[f], off[r]
         v.tensor_tensor(T.yo[:, o:o + n], T.yl[:, a:a + n], T.yl[:, b:b + n], AluOpType.add).then_inc(S.yd, 1)
         nadd += 1
-    assert all(k in seen for k in range(NK) if width[k])
+    assert all(e in seen for e in range(N) if need[e])
     g.sync.wait_ge(S.yd, nadd)
     g.sync.dma_start(T.y[:], T.yo[:]).then_inc(S.st, 16)
     g.sync.wait_ge(S.st, 16)

from concourse.bass import DstId, RemoteDMATransfer
from concourse.mybir import dt, AluOpType, ActivationFunctionType

N, NC, ALL = 12, 256, 256
S2 = 2
SLOTS = 9
GAIN = 0.019
BYTES = dt.uint8
Q8, U8, BF, F4 = "float8_e4m3fn_x4", "uint8", "bfloat16", "float32"
SCRATCH = {
    "xt": ("sbuf", [128, 4 * 384], BF),
    "xq": ("sbuf", [128, 384], Q8), "xp": ("sbuf", [128, 384], U8),
    "rq": ("sbuf", [128, 384], Q8), "rp": ("sbuf", [128, 384], U8),
    "lq": ("sbuf", [128, 768], Q8), "lp": ("sbuf", [128, 768], U8),
    "w1t": ("sbuf", [128, 2048], BF), "w2t": ("sbuf", [128, 512], BF),
    "wq": ("sbuf", [128, 640], Q8), "wp": ("sbuf", [128, 640], U8),
    "h0": ("sbuf", [128, 2048], BF), "hq0": ("sbuf", [128, 512], Q8), "hp0": ("sbuf", [128, 512], U8),
    "h1": ("sbuf", [128, 2048], BF), "hq1": ("sbuf", [128, 512], Q8), "hp1": ("sbuf", [128, 512], U8),
    "zp": ("psum", [128, 4096], F4),
    "pr": ("sbuf", [128, 512], F4),
    "yl": ("sbuf", [128, 512], F4),
    "yo": ("sbuf", [128, 256], F4),
    "gd": ("dram", [128, 4], BF), "gf": ("dram", [128, 4], BF),
    "gr": ("sbuf", [128, 512], BF), "gw": ("sbuf", [128, 512], BF),
}
for _i in range(SLOTS):
    SCRATCH["gi%d" % _i] = ("dram", [128, 4], BF)
SEMAPHORES = (["lx", "lw1", "lw2", "ld", "lg", "gb", "gf", "ga", "qx", "qo", "qw", "rc", "rp",
               "xa0", "xa1", "w", "ls", "yd", "st", "hv0", "hs0", "hq0", "p0", "hv1", "hs1", "hq1", "p1", "ev0", "ev1", "ev2"]
              + ["z%d%d" % (b, i) for b in range(2) for i in range(4)] + ["y%d" % k for k in range(N)])
CACHE = {}


def bits(mask):
    return [1 << b for b in range(mask.bit_length()) if mask >> b & 1]


def codes(ap):
    return ap.bitcast(BYTES)


def up16(v):
    return (v + 15) // 16 * 16


def plan(T, topo):
    if CACHE:
        return CACHE
    cores, cnt = list(T.cores), T.tables["CNT"]
    off = [[sum(c[:e]) for e in range(N + 1)] for c in cnt]

    def same_chip(a, b):
        return (topo.host(a), topo.chip(a)) == (topo.host(b), topo.chip(b))

    def owner(c):
        return all(topo.may_write(c, d) for d in cores if d != c)

    def helpers(c):
        hs = [d for d in range(ALL) if same_chip(c, d) and d not in cores and topo.die(d) == topo.die(c)]
        return sorted(hs, key=lambda d: (not owner(d), d))

    start, width, runs, need, wrap = [], [], [], [], []
    for c, o in zip(cnt, off):
        both = [e for e in range(S2) if c[e] and c[e - S2]]
        wr = sum(c[both[0] - S2:]) if both else 0
        st, wd, rn = [], [], []
        for e in range(N):
            f = (e - S2) % N
            pf = wr + o[f] - (NC if e in both else 0)
            s = pf if c[f] else wr + o[e]
            end = wr + o[e + 1] if c[e] else s + c[f]
            st.append(s)
            wd.append(end - s)
            rn.append([(w, r, p, c[r]) for w, r, p in ((1, f, 0), (0, e, end - s - c[e])) if c[r]])
        start.append(st)
        width.append(wd)
        runs.append(rn)
        need.append([c[e - S2] + c[e] for e in range(N)])
        wrap.append(wr)
    tot = [NC + w for w in wrap]
    pos = [[sum(need[j][:e]) for e in range(N)] for j in range(N)]

    comp, dest, team = {}, {}, {}
    dies = sorted({topo.die(c) for c in cores})
    entry = {(k, x): 0 for k in range(N // 2) for x in dies}
    for e in range(N):
        c = cores[e]
        team[e] = [c] + [helpers(d)[0] for d in cores if same_chip(c, d) and topo.die(d) != topo.die(c)]
        if 2 * sum(topo.may_write(c, d) for d in cores if d != c) < N:
            team[e].append(helpers(c)[1])
    for turn in range(3):
        for e in range(N):
            cc = team[e]
            others = sorted([j for j in range(N) if j != e and need[j][e]], key=lambda j: -width[j][e])
            load, num = {d: 0 for d in cc}, {d: 0 for d in cc}
            load[cores[e]] = width[e][e]
            best, pick = [10 ** 9, None], {}

            def count(j, d, s):
                load[d] += s * width[j][e]
                num[d] += s
                if not same_chip(d, cores[j]):
                    entry[j // 2, topo.die(d)] += s * need[j][e]
            if turn:
                for j in others:
                    entry[j // 2, topo.die(dest[j, e])] -= 0 if same_chip(cores[e], cores[j]) else need[j][e]

            def search(i):
                if max(load[d] + 16 * num[d] for d in cc) >= best[0]:
                    return
                if i == len(others):
                    cost = (max(load[d] + 16 * num[d] for d in cc)
                            + sum(abs(entry[k, dies[0]] - entry[k, dies[1]]) for k in range(N // 2)) // 4)
                    if cost < best[0] and all(128 <= load[d] <= 512 for d in cc[1:]):
                        best[0], best[1] = cost, dict(pick)
                    return
                j = others[i]
                for d in cc:
                    if num[d] < SLOTS and topo.may_write(d, cores[j]):
                        pick[j] = d
                        count(j, d, 1)
                        search(i + 1)
                        count(j, d, -1)
            search(0)
            for d in cc:
                comp[d] = {"e": e, "own": e if d == cores[e] else None, "from": [j for j in others if best[1][j] == d]}
            for j in others:
                dest[j, e] = best[1][j]
                entry[j // 2, topo.die(dest[j, e])] += 0 if same_chip(cores[e], cores[j]) else need[j][e]

    via, relay = {}, {}
    for j in range(N):
        c = cores[j]
        hs = helpers(c)[:3]
        away = [e for e in range(N) if (j, e) in dest]
        near = [e for e in away if same_chip(dest[j, e], c)]
        cross = [e for e in away if e not in near and not all(topo.may_write(s, dest[j, e]) for s in [c] + hs)]
        own = [s for s in hs + [c] if all(topo.may_write(s, dest[j, e]) for e in cross)]
        num = {s: 0 for s in [c] + hs}
        for e in near:
            via[j, e] = c
            num[c] += 0.5
        for i, e in enumerate(cross):
            s = own[i * len(own) // len(cross)]
            via[j, e] = s
            num[s] += 1
        rest, order = [e for e in away if (j, e) not in via], [s for s in hs if s not in own] + [c] + [s for s in own if s != c]
        level = 1
        while sum(max(0, int(level - num[s])) for s in order) < len(rest):
            level += 0.5
        for s in order:
            while rest and num[s] + 1 <= level:
                via[j, rest.pop(0)] = s
                num[s] += 1
        assert not rest
        relay[j] = [h for h in hs if num[h]]
        relay[j].sort(key=lambda h: -num[h])

    send = {}
    for d, q in comp.items():
        e, own, col, land = q["e"], q["own"], 0, []
        q["lo"] = 0
        if own is not None:
            w, s = width[own][e], start[own][e]
            m = max(128, up16(w))
            ahead = s + w >= m
            if ahead:
                q["fill"], q["lo"], col = (0, s + w - m, m), m - w, m
                if w:
                    land.append((own, m - w))
        for i, j in enumerate(q["from"]):
            s, n, lead = start[j][e], width[j][e], 0
            if own is not None and not ahead and i == len(q["from"]) - 1 and (col + n) % 16:
                lead = 0 if s + n + 8 <= tot[j] else 8
                s, n = s - lead, n + 8
            send[j, e] = (s, n, col)
            land.append((j, col + lead))
            col += n
        if own is not None and not ahead:
            s, n = start[own][e], width[own][e]
            q["fill"] = (col, s, max(128, up16(n)))
            assert col % 16 == 0 and s + q["fill"][2] <= tot[own]
            if n:
                land.append((own, col))
            col = max(128, col + n)
        q["lo"] = min(q["lo"], max(0, col - 128))
        q["n"] = n = col - q["lo"]
        assert 128 <= n <= 512
        q["land"] = land = [(j, c - q["lo"]) for j, c in land]
        q["ans"] = {j: sum(need[i][e] for i, _ in land[:k]) for k, (j, _) in enumerate(land)}
        mid = min([c for j, c in land if c >= 128] or [n], key=lambda c: abs(c - n // 2))
        two = n - mid >= 48
        q["batches"] = [(0, mid), (min(mid, n - 128), max(128, n - mid))] if two else [(0, n)]
        q["batch"] = {j: int(two and c >= mid) for j, c in land}

    span, skip = {}, {}
    for j in range(N):
        span[j] = []
        for h in relay[j]:
            es = [e for e in range(N) if via.get((j, e)) == h]
            lo = min(send[j, e][0] for e in es)
            hi = max(send[j, e][0] + send[j, e][1] for e in es)
            span[j].append((h, lo, hi))
            for e in es:
                skip[j, e] = send[j, e][0] - lo

    CACHE.update(cores=cores, cnt=cnt, off=off, need=need, runs=runs, pos=pos, tot=tot, wrap=wrap, comp=comp, dest=dest, via=via,
                 send=send, span=span, skip=skip, entry=entry)
    return CACHE


def weight_dests(core, P):
    e = P["comp"][core]["e"]
    return [d for d, q in P["comp"].items() if q["e"] == e and d != core]


def engine_halves(core, P, topo):
    out = [d for d in P["cores"] if d != core and topo.may_write(core, d)
           and (topo.host(d), topo.chip(d)) != (topo.host(core), topo.chip(core))][0]
    lo = bits(topo.mask(core, out))
    return lo, [b for b in bits(topo.mask(core, weight_dests(core, P)[0])) if b not in lo]


def rank_program(g, core, T, topo):
    P = plan(T, topo)
    rank, sent = T.rank_of(core), [0]

    def push(dst, out, src, sem):
        m = topo.mask(core, dst)
        rid, pid = topo.addr(dst, core)
        g.remote_dma(out, src, sem, T.sem.ls, pid, rid, m)
        sent[0] += len(bits(m))

    def fused(items):
        tr = []
        for dsts, src, sem, eng in items:
            ids = []
            for d, o in dsts:
                rid, pid = topo.addr(d, core)
                ids.append(DstId(rid=rid, pnc=pid))
            tr.append(RemoteDMATransfer(dst_ids=ids, dma_engine_mask=sum(eng), remote_sem=sem, srcs=[src], dsts=[o for d, o in dsts]))
            sent[0] += len(eng)
        g.remote_dma_fused(tr, local_sem=T.sem.ls)

    if rank is not None:
        send_side(g, core, rank, T, P, push, fused, topo)
    helping = [(j, e) for (j, e), h in P["via"].items() if h == core and j != rank]
    if helping:
        relay_side(g, core, T, P, helping, push, fused, topo)
    if core in P["comp"]:
        compute_side(g, core, rank, T, P, push, topo)
    if rank is not None:
        combine_side(g, rank, T, P, topo)
    if sent[0]:
        g.wait_ge(T.sem.ls, sent[0])


def gate_slots(T, P, j, core):
    return [(P["dest"][j, e], T["gi%d" % P["comp"][P["dest"][j, e]]["from"].index(j)][:])
            for e in range(N) if P["via"].get((j, e)) == core]


def window_to(T, P, j, e, push, q, p, a):
    (_, w, c), d = P["send"][j, e], P["dest"][j, e]
    sem = T.sem["xa%d" % P["comp"][d]["batch"][j]]
    push(d, codes(T.lq[:, c:c + w]), codes(q[:, a:a + w]), sem)
    push(d, T.lp[:, c:c + w], p[:, a:a + w], sem)


def send_side(g, core, rank, T, P, push, fused, topo):
    S, tot, wrap, v = T.sem, P["tot"][rank], P["wrap"][rank], g.vector
    g.scalar.dma_start(T.gd[:], T.gt[:]).then_inc(S.ld, 16)
    g.sync.dma_start(T.xt[:, 4 * wrap:4 * tot], T.x[:]).then_inc(S.lx, 16)
    if wrap:
        g.sync.dma_start(T.xt[:, 0:4 * wrap], T.x[:, 4 * (NC - wrap):4 * NC]).then_inc(S.lx, 16)
    g.sync.dma_start(T.w1t[:], T.w1[:]).then_inc(S.lw1, 16)
    g.sync.dma_start(T.w2t[:], T.w2[:]).then_inc(S.lw2, 16)

    v.wait_ge(S.lx, 32 if wrap else 16)
    v.quantize_mx(T.xq[:, 0:tot], T.xp[:, 0:tot], T.xt[:, 0:4 * tot]).then_inc(S.qx, 1)
    p, s, m = P["comp"][core]["fill"]
    v.quantize_mx(T.lq[:, p:p + m], T.lp[:, p:p + m], T.xt[:, 4 * s:4 * (s + m)]).then_inc(S.qo, 1)
    v.wait_ge(S.lw1, 16)
    v.quantize_mx(T.wq[:, 0:512], T.wp[:, 0:512], T.w1t[:]).then_inc(S.qw, 1)
    v.wait_ge(S.lw2, 16)
    v.quantize_mx(T.wq[:, 512:640], T.wp[:, 512:640], T.w2t[:]).then_inc(S.qw, 1)

    lo, hi = engine_halves(core, P, topo)
    sp = P["span"][rank]
    g.wait_ge(S.ld, 16)
    far, near = gate_slots(T, P, rank, core), [(h, T.gf[:]) for h, a, b in sp]
    fused(([(far, T.gd[:], S.ga, lo)] if far else []) + ([(near, T.gd[:], S.gf, hi)] if near else []))
    g.wait_ge(S.qx, 1)
    for h, a, b in sp:
        push(h, codes(T.rq[:, 0:b - a]), codes(T.xq[:, a:b]), S.rc)
        push(h, T.rp[:, 0:b - a], T.xp[:, a:b], S.rp)
    for e in range(N):
        if P["via"].get((rank, e)) == core:
            window_to(T, P, rank, e, push, T.xq, T.xp, P["send"][rank, e][0])
    g.wait_ge(S.qw, 2)
    ds = weight_dests(core, P)
    fused([([(d, codes(T.wq[:]))], codes(T.wq[:]), S.w, eng) for d, eng in zip(ds, (hi, lo))])
    fused([([(d, T.wp[:])], T.wp[:], S.w, eng) for d, eng in zip(ds, (lo, hi))])


def relay_side(g, core, T, P, helping, push, fused, topo):
    S, j = T.sem, helping[0][0]
    src = P["cores"][j]
    lo, hi = engine_halves(src, P, topo)
    n = len(bits(topo.mask(src, core)))
    g.wait_ge(S.gf, len(hi))
    fused([(gate_slots(T, P, j, core), T.gf[:], S.ga, lo)])
    g.wait_ge(S.rc, n)
    g.wait_ge(S.rp, n)
    for j, e in helping:
        window_to(T, P, j, e, push, T.rq, T.rp, P["skip"][j, e])


def compute_side(g, core, rank, T, P, push, topo):
    S, q, cores = T.sem, P["comp"][core], P["cores"]
    e, lo, bat, ans = q["e"], q["lo"], q["batches"], q["ans"]
    te, ve, sc = g.tensor, g.vector, g.scalar
    num = 0
    for j, c in sorted(q["land"], key=lambda t: t[0] != rank):
        if j == rank:
            src = T.gd
            g.sync.wait_ge(S.ld, 16)
        else:
            src = T["gi%d" % q["from"].index(j)]
            if j == q["from"][0]:
                g.sync.wait_ge(S.ga, sum(len(engine_halves(cores[i], P, topo)[0]) for i in q["from"]))
        k = ans[j]
        for which, r, p, m in P["runs"][j][e]:
            row = (NC * which + P["off"][j][r]) // 4
            g.sync.dma_start(T.gr[0:1, k:k + m], src[row:row + m // 4, :]).then_inc(S.lg, 16)
            k += m
            num += 1
    if rank is not None:
        te.wait_ge(S.qw, 2)
        te.wait_ge(S.qo, 1)
    else:
        te.wait_ge(S.w, sum(len(b) for b in engine_halves(cores[e], P, topo)))
    for b, (a, m) in enumerate(bat):
        arr = sum(2 * len(bits(topo.mask(P["via"][j, e], core))) for j in q["from"] if q["batch"][j] == b)
        if arr:
            te.wait_ge(S["xa%d" % b], arr)
        x, xs = T.lq[:, lo + a:lo + a + m], T.lp[:, lo + a:lo + a + m]
        for i in range(4):
            o = 512 * (4 * b + i)
            te.matmul_mx(T.zp[:, o:o + m], T.wq[:, 128 * i:128 * i + 128], T.wp[:, 128 * i:128 * i + 128], x, xs, True, True).then_inc(S["z%d%d" % (b, i)], 1)
    for b, (a, m) in enumerate(bat):
        h, hq, hp = T["h%d" % b], T["hq%d" % b], T["hp%d" % b]
        for i in range(4):
            o = 512 * (4 * b + i)
            out, z, sem = h[:, i:4 * m:4], T.zp[:, o:o + m], S["z%d%d" % (b, i)]
            if i % 2 == b:
                ve.wait_ge(sem, 1)
                ve.tensor_scalar(out, z, 0.0, GAIN, AluOpType.max, AluOpType.mult).then_inc(S["hv%d" % b], 1)
            else:
                sc.wait_ge(sem, 1)
                sc.activation(out, z, ActivationFunctionType.Relu, scale=GAIN).then_inc(S["hs%d" % b], 1)
        ve.wait_ge(S["hv%d" % b], 2)
        ve.wait_ge(S["hs%d" % b], 2)
        ve.quantize_mx(hq[:, 0:m], hp[:, 0:m], h[:, 0:4 * m]).then_inc(S["hq%d" % b], 1)
        te.wait_ge(S["hq%d" % b], 1)
        te.matmul_mx(T.zp[:, 2048 * b:2048 * b + m], T.wq[:, 512:640], T.wp[:, 512:640], hq[:, 0:m], hp[:, 0:m], True, True).then_inc(S["p%d" % b], 1)
    end = sum(P["need"][j][e] for j, c in q["land"])
    g.wait_ge(S.lg, 16 * num)
    g.partition_broadcast(T.gw[:, 0:end], T.gr[0:1, 0:end], 128).then_inc(S.gb, 1)
    ve.wait_ge(S.gb, 1)
    for b, (a, m) in enumerate(bat):
        def gated(out, k, src, m):
            o = 2048 * b + src - a
            return ve.tensor_tensor(out, T.zp[:, o:o + m], T.gw[:, k:k + m], AluOpType.mult)
        ve.wait_ge(S["p%d" % b], 1)
        grp, calls = [t for t in q["land"] if t[0] != rank and q["batch"][t[0]] == b], []
        for j, c in grp:
            k = ans[j]
            for _, r, p, m in P["runs"][j][e]:
                if calls and calls[-1][0] + calls[-1][2] == k and calls[-1][1] + calls[-1][2] == c + p:
                    calls[-1][2] += m
                else:
                    calls.append([k, c + p, m])
                k += m
        for k, src, m in calls:
            gated(T.pr[:, k:k + m], k, src, m).then_inc(S["ev%d" % b], 1)
        if grp:
            g.wait_ge(S["ev%d" % b], len(calls))
        for j, c in grp:
            k, o, m = ans[j], P["pos"][j][e], P["need"][j][e]
            push(cores[j], T.yl[:, o:o + m], T.pr[:, k:k + m], S["y%d" % e])
        for j, c in q["land"]:
            if j == rank and q["batch"][j] == b:
                k, o = ans[j], P["pos"][j][e]
                for _, r, p, m in P["runs"][j][e]:
                    gated(T.yl[:, o:o + m], k, c + p, m).then_inc(S.ev2, 1)
                    k, o = k + m, o + m
                ve.wait_ge(S.ev2, len(P["runs"][j][e]))


def combine_side(g, rank, T, P, topo):
    S, v, cnt, off, cores = T.sem, g.vector, P["cnt"][rank], P["off"][rank], P["cores"]
    need, pos = P["need"][rank], P["pos"][rank]

    def due(e):
        if e == rank or not need[e]:
            return -1
        q = P["comp"][P["dest"][rank, e]]
        return q["from"].index(rank) + q["n"] / 100
    seen, nadd = [rank], 0
    for r in sorted(range(N), key=lambda r: max(due(r), due((r + S2) % N))):
        n, f = cnt[r], (r + S2) % N
        if not n:
            continue
        for e in sorted((r, f), key=due):
            if e not in seen:
                v.wait_ge(S["y%d" % e], len(bits(topo.mask(P["dest"][rank, e], cores[rank]))))
                seen.append(e)
        a, b, o = pos[r] + cnt[r - S2], pos[f], off[r]
        v.tensor_tensor(T.yo[:, o:o + n], T.yl[:, a:a + n], T.yl[:, b:b + n], AluOpType.add).then_inc(S.yd, 1)
        nadd += 1
    assert all(e in seen for e in range(N) if need[e])
    g.sync.wait_ge(S.yd, nadd)
    g.sync.dma_start(T.y[:], T.yo[:]).then_inc(S.st, 16)
    g.sync.wait_ge(S.st, 16)
